import numpy as np, ml_dtypes
CORES = [23,119,17,113]
N = 4
import mx_ref
NC, G, MB = 256, 2, 2
C = np.float32(0.041)
BF = ml_dtypes.bfloat16
def cut(t, i, w=512):
    return t[:, w * i:w * i + w]
def tile(rs):
    return np.stack(rs, axis=2).reshape(128, -1).astype(BF)
def layer(w, X):
    out = []
    for i in range(G):
        for t in range(len(X)):
            p = mx_ref.matmul(mx_ref.quantize(cut(w, len(X) * i + t)), X[t])
            z = p if t == 0 else z + p
        out.append(z)
    return out
def act(Z):
    return [np.maximum(s * z, 0) * C for z in Z for s in (1, -1)]
def setup_inputs(rng):
    def f(*shape):
        return mx_ref.flush((rng.standard_normal(shape, dtype=np.float32) * np.exp2(rng.integers(-2, 3, shape[:-1] + (1,)))).astype(BF))
    return {"x": f(N, 128, 4 * NC), "w1": f(N, 128, G * 512), "w2": f(N, 128, 512), "px": f(N, 128, MB * 4 * NC), "pw": f(N, 128, G * 512)}
def setup_inputs_blocks(rng):
    d = setup_inputs(rng)
    for k in ("x", "w1", "w2", "px"): d[k] = mx_ref.spread(d[k], rng, 4)
    for k in ("pw",): d[k] = mx_ref.spread(d[k], rng, 1)
    return d
def setup_inputs_wide(rng):
    d = setup_inputs(rng)
    for k in ("x", "w1", "w2", "px"): d[k] = mx_ref.flush((d[k].astype(np.float32) * np.exp2(rng.integers(-6, 7, (N, 1, 1))).astype(np.float32)).astype(BF))
    return d
def setup_inputs_zeros(rng):
    d = setup_inputs(rng); v = d["x"].reshape(N, 128, -1, 4).copy()
    v[np.broadcast_to((rng.random((N, 1, v.shape[2], 1)) < 0.33), v.shape)] = 0
    d["x"] = v.reshape(d["x"].shape)
    return d
def reference(x, w1, w2, px, pw):
    H = [mx_ref.quantize(tile(act(layer(w1[j], [mx_ref.quantize(x[j])])))) for j in range(N)]
    y = np.zeros((N, 128, N * NC), np.float32)
    for r in range(N):
        qw = mx_ref.quantize(w2[r])
        for j in range(N):
            y[r][:, NC * j:NC * j + NC] = mx_ref.matmul(qw, H[j])
    z = np.full((N, 128, MB * G * NC), np.nan, np.float32)
    for m in range(MB):
        a = mx_ref.quantize(cut(px[N - 1], m, 4 * NC))
        for s in range(N - 1):
            a = mx_ref.quantize(tile(act(layer(pw[s], [a]))))
        Z = layer(pw[N - 1], [a])
        for i in range(G):
            z[N - 1][:, NC * (G * m + i):NC * (G * m + i) + NC] = Z[i]
    return {"y": y, "z": z}

@@ -1,0 +1,324 @@
+import numpy as np
+from concourse.bass import DstId, RemoteDMATransfer
+from concourse.mybir import dt, AluOpType, ActivationFunctionType
+
+NC = 256
+HC = NC // 2
+SC = 128
+G = 2
+C = float(np.float32(0.041))
+FIRST, LAST = 0, 3
+MIDDLE = {0: 2, 1: 1}
+HUBS = (0, 3)
+CFG = {"all": 1, "hold": 1, "ldhold": 1, "runs": [(0, NC), (NC, 2 * NC)], "pre": {1: 2, 2: 2},
+       "Q": ["w", "w"], "R": ["c", "c"]}
+
+CODES = "float8_e4m3fn_x4"
+SCRATCH = {
+    "tx": ("sbuf", [128, 4 * NC], "bfloat16"),
+    "tw1": ("sbuf", [128, G * 512], "bfloat16"),
+    "tw2": ("sbuf", [128, 512], "bfloat16"),
+    "tpx": ("sbuf", [128, 2 * 4 * NC], "bfloat16"),
+    "tpw": ("sbuf", [128, G * 512], "bfloat16"),
+    "th": ("sbuf", [128, 4 * NC], "bfloat16"),
+    "ta": ("sbuf", [128, 4 * NC], "bfloat16"),
+    "tb": ("sbuf", [128, 4 * NC], "bfloat16"),
+    "oy": ("sbuf", [128, 4 * NC], "float32"),
+    "oz": ("sbuf", [128, 4 * NC], "float32"),
+    "ps": ("psum", [128, 8 * 512], "float32"),
+}
+for _n, _w in (("x", NC), ("w1", G * SC), ("w2", SC), ("pw", G * SC), ("lw", G * SC), ("px", 2 * NC), ("lp", 2 * NC),
+               ("h", 4 * NC), ("a", 2 * NC), ("b", NC), ("la", NC), ("lz", 2 * NC)):
+    SCRATCH["q" + _n] = ("sbuf", [128, _w], CODES)
+    SCRATCH["s" + _n] = ("sbuf", [128, _w], "uint8")
+
+SEMAPHORES = (["ld_" + n for n in ("x", "w1", "w2", "px0", "px1", "px2", "pw")]
+              + ["q_" + n for n in ("x", "w1", "w2", "px0", "px1", "px2", "pw")]
+              + ["hn", "hf", "lw", "sent", "sent2", "st_sync", "st_scalar"]
+              + ["%s%d%d" % (s, m, h) for s in ("lp", "la", "lz") for m in range(2) for h in range(2)]
+              + ["%s_%s" % (s, e) for s in ("h", "a00", "a01", "a10", "a11", "b00", "b01")
+                 for e in ("z0", "z1", "act", "q")]
+              + ["y%d_%s" % (j, e) for j in range(4) for e in ("z", "c")]
+              + ["z%d%d_%s" % (j, h, e) for j in range(4) for h in range(2) for e in ("z", "c")])
+
+
+def rank_program(g, core, T, topo):
+    rank = T.rank_of(core)
+    if rank is None:
+        return
+    sem, cores = T.sem, T.cores
+    te, ve, sc, sy = g.tensor, g.vector, g.scalar, g.sync
+    RELU, COPY = ActivationFunctionType.Relu, ActivationFunctionType.Copy
+    MAX, MULT = AluOpType.max, AluOpType.mult
+    ranks = range(len(cores))
+
+    def same_chip(r, s):
+        return topo.chip(cores[r]) == topo.chip(cores[s])
+
+    mate = [r for r in ranks if r != rank and same_chip(r, rank)][0]
+    far = [r for r in ranks if not same_chip(r, rank)]
+    place = sorted(ranks, key=lambda r: (topo.chip(cores[r]), r))
+    pos = {r: NC * place.index(r) for r in ranks}
+    sent = {"sent": 0, "sent2": 0}
+
+    def bank(k, n):
+        return T.ps[:, 512 * k:512 * k + n]
+
+    def pair(name, a, b):
+        return T["q" + name][:, a:b], T["s" + name][:, a:b]
+
+    def count(mask):
+        return bin(mask).count("1")
+
+    def mask_of(s, d, everything=False):
+        m = topo.mask(cores[s], cores[d])
+        if same_chip(s, d) and not everything:
+            m &= ~topo.mask(cores[s], cores[[r for r in ranks if not same_chip(r, s)][0]])
+        return m
+
+    def part(kind, d, dst, src, done, everything=False, local="sent"):
+        rid, pid = topo.addr(cores[d])[:2]
+        m = mask_of(rank, d, everything)
+        (dn, da, db), (sn, sa, sb) = dst, src
+        out, in_ = T[kind + dn][:, da:db], T[kind + sn][:, sa:sb]
+        if kind == "q":
+            out, in_ = out.bitcast(dt.uint8), in_.bitcast(dt.uint8)
+        g.remote_dma(out, in_, sem[done], sem[local], pid, rid, m)
+        sent[local] += count(m)
+
+    def arrival(s, parts=2, everything=False):
+        return parts * count(mask_of(s, rank, everything))
+
+    def hop(mode, d, dname, da, sname, sa, done, ready):
+        def p(kind, a, b, h):
+            part(kind, d, (dname, da + a, da + b), (sname, sa + a, sa + b), done + str(h), CFG["all"])
+        if mode == "w":
+            for r in ready:
+                g.wait_ge(sem[r], 1)
+            p("q", 0, NC, 0)
+            p("s", 0, NC, 0)
+        elif mode == "c":
+            for h in range(2):
+                g.wait_ge(sem[ready[h]], 1)
+                p("q", HC * h, HC * h + HC, 0)
+            p("s", 0, NC, 0)
+        else:
+            for h in range(2):
+                g.wait_ge(sem[ready[h]], 1)
+                p("q", HC * h, HC * h + HC, h)
+                p("s", HC * h, HC * h + HC, h)
+
+    def await_half(mode, s, name, h):
+        if mode == "h":
+            te.wait_ge(sem[name + str(h)], arrival(s, 2, CFG["all"]))
+        elif h == 0:
+            te.wait_ge(sem[name + "0"], arrival(s, {"w": 2, "c": 3}[mode], CFG["all"]))
+
+    def send_h():
+        hub = [r for r in HUBS if r in far][0]
+        a, b = pos[rank], pos[rank] + NC
+        for k in range(2):
+            def v():
+                return T.qh[:, a:b].bitcast(dt.uint8) if k == 0 else T.sh[:, a:b]
+            trs = []
+            for d, done in ((hub, "hf"), (mate, "hn")):
+                rid, pid = topo.addr(cores[d])[:2]
+                m = mask_of(rank, d)
+                trs.append(RemoteDMATransfer(dst_ids=[DstId(rid=rid, pnc=pid)], dma_engine_mask=m,
+                                             remote_sem=sem[done], srcs=[v()], dsts=[v()]))
+                sent["sent"] += count(m)
+            g.remote_dma_fused(trs, local_sem=sem["sent"])
+
+    def relay_h(local):
+        a = min(pos[r] for r in far)
+        g.wait_ge(sem["hf"], sum(arrival(r) for r in far))
+        for kind in "qs":
+            part(kind, mate, ("h", a, a + 2 * NC), ("h", a, a + 2 * NC), "hf", True, local)
+
+    def load(name, tile, src):
+        sy.dma_start(tile, src).then_inc(sem["ld_" + name], 16)
+
+    def quant(name, t, a, b, tag=None):
+        tag = tag or name
+        ve.wait_ge(sem["ld_" + tag], 16)
+        q, p = pair(name, a, b)
+        ve.quantize_mx(q, p, t[:, 4 * a:4 * b]).then_inc(sem["q_" + tag], 1)
+
+    def mm(k, n, w, i, m, ev):
+        wq, wp = pair(w, SC * i, SC * i + SC)
+        te.matmul_mx(bank(k, n), wq, wp, m[0], m[1], True, True).then_inc(sem[ev], 1)
+
+    def act(ev, b0, b1, n, t, a, out, oa):
+        def v(b):
+            return t[:, 4 * a + b:4 * (a + n):4]
+        sc.wait_ge(sem[ev + "_z0"], 1)
+        sc.activation(v(0), bank(b0, n), RELU, scale=C).then_inc(sem[ev + "_act"], 1)
+        sc.activation(v(1), bank(b0, n), RELU, scale=-C).then_inc(sem[ev + "_act"], 1)
+        ve.wait_ge(sem[ev + "_z1"], 1)
+        ve.tensor_scalar(v(2), bank(b1, n), 0.0, C, MAX, MULT).then_inc(sem[ev + "_act"], 1)
+        ve.tensor_scalar(v(3), bank(b1, n), -C, 0.0, MULT, MAX).then_inc(sem[ev + "_act"], 1)
+        ve.wait_ge(sem[ev + "_act"], 4)
+        q, p = pair(out, oa, oa + n)
+        ve.quantize_mx(q, p, t[:, 4 * a:4 * (a + n)]).then_inc(sem[ev + "_q"], 1)
+
+    def stage(ev, w, src, sa, before, bks, t, out, oa):
+        for h in range(2):
+            before(h)
+            s = pair(src, sa + HC * h, sa + HC * h + HC)
+            for i in range(G):
+                mm(bks[2 * h + i], HC, w, i, s, "%s%d_z%d" % (ev, h, i))
+            act("%s%d" % (ev, h), bks[2 * h], bks[2 * h + 1], HC, t, HC * h, out, oa + HC * h)
+
+    def make_h():
+        te.wait_ge(sem["q_x"], 1)
+        te.wait_ge(sem["q_w1"], 1)
+        for i in range(G):
+            mm(i, NC, "w1", i, pair("x", 0, NC), "h_z%d" % i)
+        act("h", 0, 1, NC, T.th, 0, "h", pos[rank])
+        g.wait_ge(sem["h_q"], 1)
+        send_h()
+
+    stores = [0]
+    yrow = [rank, mate] + far
+
+    def make_y(lo, hi, banks):
+        for k in range(lo, hi):
+            j = yrow[k]
+            if k == 0:
+                te.wait_ge(sem["q_w2"], 1)
+                te.wait_ge(sem["h_q"], 1)
+            elif k == 1:
+                te.wait_ge(sem["hn"], arrival(mate))
+            elif k == 2:
+                te.wait_ge(sem["hf"], sum(arrival(r) for r in far) if rank in HUBS else arrival(mate, 2, True))
+            mm(banks[k], NC, "w2", 0, pair("h", pos[j], pos[j] + NC), "y%d_z" % j)
+            out = T.oy[:, NC * j:NC * j + NC]
+            (sc, ve)[k % 2].wait_ge(sem["y%d_z" % j], 1)
+            if k % 2 == 0:
+                sc.activation(out, bank(banks[k], NC), COPY).then_inc(sem["y%d_c" % j], 1)
+            else:
+                ve.tensor_copy(out, bank(banks[k], NC)).then_inc(sem["y%d_c" % j], 1)
+            sy.wait_ge(sem["y%d_c" % j], 1)
+            sy.dma_start(T.y[:, NC * j:NC * j + NC], out).then_inc(sem["st_sync"], 16)
+            stores[0] += 16
+
+    def hold():
+        if CFG["hold"]:
+            sy.wait_ge(sem["sent"], sent["sent"])
+
+    def wait_y(ks):
+        for k in ks:
+            te.wait_ge(sem["y%d_c" % yrow[k]], 1)
+
+    if rank == FIRST:
+        load("x", T.tx[:], T.x[:])
+        load("w1", T.tw1[:], T.w1[:])
+        load("pw", T.tpw[:], T.pw[:])
+        load("w2", T.tw2[:], T.w2[:])
+        quant("x", T.tx, 0, NC)
+        quant("w1", T.tw1, 0, G * SC)
+        make_h()
+        quant("pw", T.tpw, 0, G * SC)
+        quant("w2", T.tw2, 0, SC)
+        te.wait_ge(sem["q_pw"], 1)
+        for m in range(2):
+            if m == 1:
+                te.wait_ge(sem["h_act"], 4)
+
+            def before(h):
+                if h == 0:
+                    te.wait_ge(sem["lp%d0" % m], arrival(LAST, (len(CFG["runs"]), 1)[m]))
+            stage("a%d" % m, "pw", "lp", NC * m, before, ([2, 3, 4, 5], [6, 7, 0, 1])[m], (T.ta, T.tb)[m], "a", NC * m)
+            hop(CFG["Q"][m], MIDDLE[m], "la", 0, "a", NC * m, "la0", ["a%d0_q" % m, "a%d1_q" % m])
+        hold()
+        relay_h("sent2")
+        for h in range(2):
+            te.wait_ge(sem["a0%d_act" % h], 4)
+        make_y(0, 4, [2, 3, 4, 5])
+    elif rank != LAST:
+        m = [t for t in MIDDLE if MIDDLE[t] == rank][0]
+        other = MIDDLE[1 - m]
+        load("pw", T.tpw[:], T.pw[:])
+        load("x", T.tx[:], T.x[:])
+        load("w1", T.tw1[:], T.w1[:])
+        load("w2", T.tw2[:], T.w2[:])
+        quant("pw", T.tpw, 0, G * SC)
+        g.wait_ge(sem["q_pw"], 1)
+        for kind in "qs":
+            part(kind, other, ("lw", 0, G * SC), ("pw", 0, G * SC), "lw")
+        quant("x", T.tx, 0, NC)
+        quant("w1", T.tw1, 0, G * SC)
+        make_h()
+        quant("w2", T.tw2, 0, SC)
+        pre = CFG["pre"][rank]
+        te.wait_ge(sem["h_act"], 4)
+        make_y(0, pre, [2, 3, 4, 5])
+        w = ["pw", "lw"] if rank == 1 else ["lw", "pw"]
+        te.wait_ge(sem["q_pw"], 1)
+        te.wait_ge(sem["lw"], arrival(other))
+        stage("a0", w[0], "la", 0, lambda h: await_half(CFG["Q"][m], FIRST, "la0", h), [6, 7, 0, 1], T.ta, "a", 0)
+        wait_y(range(pre))
+        stage("b0", w[1], "a", 0, lambda h: te.wait_ge(sem["a0%d_q" % h], 1), [2, 3, 4, 5], T.tb, "b", 0)
+        hop(CFG["R"][m], LAST, "lz", NC * m, "b", 0, "lz%d" % m, ["b00_q", "b01_q"])
+        hold()
+        make_y(pre, 4, [6, 7, 0, 1])
+    else:
+        runs = CFG["runs"]
+        for k, (a, b) in enumerate(runs):
+            load("px%d" % k, T.tpx[:, 4 * a:4 * b], T.px[:, 4 * a:4 * b])
+        load("x", T.tx[:], T.x[:])
+        load("w1", T.tw1[:], T.w1[:])
+        for k, (a, b) in enumerate(runs):
+            quant("px", T.tpx, a, b, "px%d" % k)
+            g.wait_ge(sem["q_px%d" % k], 1)
+            if a == NC:
+                part("s", FIRST, ("lp", 0, 2 * NC), ("px", 0, 2 * NC), "lp00", local="sent2")
+            part("q", FIRST, ("lp", a, b), ("px", a, b), "lp%d0" % (a // NC), local="sent2")
+        if CFG["ldhold"]:
+            sy.wait_ge(sem["sent2"], sent["sent2"])
+        load("w2", T.tw2[:], T.w2[:])
+        load("pw", T.tpw[:], T.pw[:])
+        quant("x", T.tx, 0, NC)
+        quant("w1", T.tw1, 0, G * SC)
+        make_h()
+        relay_h("sent")
+        quant("w2", T.tw2, 0, SC)
+        quant("pw", T.tpw, 0, G * SC)
+        make_y(0, 4, [2, 3, 4, 5])
+        te.wait_ge(sem["q_pw"], 1)
+        te.wait_ge(sem["h_act"], 4)
+        for m in range(2):
+            mode = CFG["R"][m]
+            n, parts = (HC, 2) if mode == "h" else (NC, 1)
+            if m == 1:
+                wait_y(range(4))
+            bks = [[6, 7, 0, 1], [2, 3, 4, 5]][m]
+            for h in range(parts):
+                await_half(mode, MIDDLE[m], "lz%d" % m, h)
+                for i in range(G):
+                    a = NC * m + n * h
+                    mm(bks[2 * h + i], n, "pw", i, pair("lz", a, a + n), "z%d%d_z" % (2 * m + i, h))
+            for h in range(parts):
+                for i in range(G):
+                    k = 2 * m + i
+                    out = T.oz[:, NC * k + n * h:NC * k + n * h + n]
+                    if i == 0:
+                        sc.wait_ge(sem["z%d%d_z" % (k, h)], 1)
+                        sc.activation(out, bank(bks[2 * h + i], n), COPY).then_inc(sem["z%d%d_c" % (k, h)], 1)
+                    else:
+                        ve.wait_ge(sem["z%d%d_z" % (k, h)], 1)
+                        ve.tensor_copy(out, bank(bks[2 * h + i], n)).then_inc(sem["z%d%d_c" % (k, h)], 1)
+            for i in range(G):
+                k = 2 * m + i
+                q = sc if k == 3 else sy
+                for h in range(parts):
+                    q.wait_ge(sem["z%d%d_c" % (k, h)], 1)
+                q.dma_start(T.z[:, NC * k:NC * k + NC], T.oz[:, NC * k:NC * k + NC]).then_inc(
+                    sem["st_scalar" if k == 3 else "st_sync"], 16)
+                if k != 3:
+                    stores[0] += 16
+        sc.wait_ge(sem["st_scalar"], 16)
+    sy.wait_ge(sem["st_sync"], stores[0])
+    for name in sent:
+        if sent[name]:
+            g.wait_ge(sem[name], sent[name])

@@ -9,9 +9,8 @@ G = 2
 C = float(np.float32(0.041))
 FIRST, LAST = 0, 3
 MIDDLE = {0: 2, 1: 1}
-HUBS = (0, 3)
-CFG = {"all": 1, "hold": 1, "ldhold": 1, "runs": [(0, NC), (NC, 2 * NC)], "pre": {1: 2, 2: 2},
-       "Q": ["w", "w"], "R": ["c", "c"]}
+HUBS = (0, 1)
+CFG = {"p1": 1, "pre": {1: 3, 2: 2}, "farfirst": [1]}
 
 CODES = "float8_e4m3fn_x4"
 SCRATCH = {
@@ -34,7 +33,7 @@ for _n, _w in (("x", NC), ("w1", G * SC), ("w2", SC), ("pw", G * SC), ("lw", G *
 
 SEMAPHORES = (["ld_" + n for n in ("x", "w1", "w2", "px0", "px1", "px2", "pw")]
               + ["q_" + n for n in ("x", "w1", "w2", "px0", "px1", "px2", "pw")]
-              + ["hn", "hf", "lw", "sent", "sent2", "st_sync", "st_scalar"]
+              + ["go", "hn", "hf", "lw", "sent", "sent2", "st_sync", "st_scalar"]
               + ["%s%d%d" % (s, m, h) for s in ("lp", "la", "lz") for m in range(2) for h in range(2)]
               + ["%s_%s" % (s, e) for s in ("h", "a00", "a01", "a10", "a11", "b00", "b01")
                  for e in ("z0", "z1", "act", "q")]
@@ -70,15 +69,15 @@ def rank_program(g, core, T, topo):
     def count(mask):
         return bin(mask).count("1")
 
-    def mask_of(s, d, everything=False):
+    def mask_of(s, d, everything=True):
         m = topo.mask(cores[s], cores[d])
         if same_chip(s, d) and not everything:
             m &= ~topo.mask(cores[s], cores[[r for r in ranks if not same_chip(r, s)][0]])
         return m
 
-    def part(kind, d, dst, src, done, everything=False, local="sent"):
+    def part(kind, d, dst, src, done, local="sent"):
         rid, pid = topo.addr(cores[d])[:2]
-        m = mask_of(rank, d, everything)
+        m = mask_of(rank, d)
         (dn, da, db), (sn, sa, sb) = dst, src
         out, in_ = T[kind + dn][:, da:db], T[kind + sn][:, sa:sb]
         if kind == "q":
@@ -86,33 +85,15 @@ def rank_program(g, core, T, topo):
         g.remote_dma(out, in_, sem[done], sem[local], pid, rid, m)
         sent[local] += count(m)
 
-    def arrival(s, parts=2, everything=False):
+    def arrival(s, parts=2, everything=True):
         return parts * count(mask_of(s, rank, everything))
 
-    def hop(mode, d, dname, da, sname, sa, done, ready):
-        def p(kind, a, b, h):
-            part(kind, d, (dname, da + a, da + b), (sname, sa + a, sa + b), done + str(h), CFG["all"])
-        if mode == "w":
-            for r in ready:
-                g.wait_ge(sem[r], 1)
-            p("q", 0, NC, 0)
-            p("s", 0, NC, 0)
-        elif mode == "c":
-            for h in range(2):
-                g.wait_ge(sem[ready[h]], 1)
-                p("q", HC * h, HC * h + HC, 0)
-            p("s", 0, NC, 0)
-        else:
-            for h in range(2):
-                g.wait_ge(sem[ready[h]], 1)
-                p("q", HC * h, HC * h + HC, h)
-                p("s", HC * h, HC * h + HC, h)
-
-    def await_half(mode, s, name, h):
-        if mode == "h":
-            te.wait_ge(sem[name + str(h)], arrival(s, 2, CFG["all"]))
-        elif h == 0:
-            te.wait_ge(sem[name + "0"], arrival(s, {"w": 2, "c": 3}[mode], CFG["all"]))
+    def hop(d, dname, da, sname, sa, done, ready):
+        for h in range(2):
+            a = HC * h
+            g.wait_ge(sem[ready[h]], 1)
+            for kind in "qs":
+                part(kind, d, (dname, da + a, da + a + HC), (sname, sa + a, sa + a + HC), done + str(h))
 
     def send_h():
         hub = [r for r in HUBS if r in far][0]
@@ -123,7 +104,7 @@ def rank_program(g, core, T, topo):
             trs = []
             for d, done in ((hub, "hf"), (mate, "hn")):
                 rid, pid = topo.addr(cores[d])[:2]
-                m = mask_of(rank, d)
+                m = mask_of(rank, d, False)
                 trs.append(RemoteDMATransfer(dst_ids=[DstId(rid=rid, pnc=pid)], dma_engine_mask=m,
                                              remote_sem=sem[done], srcs=[v()], dsts=[v()]))
                 sent["sent"] += count(m)
@@ -133,7 +114,7 @@ def rank_program(g, core, T, topo):
         a = min(pos[r] for r in far)
         g.wait_ge(sem["hf"], sum(arrival(r) for r in far))
         for kind in "qs":
-            part(kind, mate, ("h", a, a + 2 * NC), ("h", a, a + 2 * NC), "hf", True, local)
+            part(kind, mate, ("h", a, a + 2 * NC), ("h", a, a + 2 * NC), "hf", local)
 
     def load(name, tile, src):
         sy.dma_start(tile, src).then_inc(sem["ld_" + name], 16)
@@ -179,18 +160,18 @@ def rank_program(g, core, T, topo):
         send_h()
 
     stores = [0]
-    yrow = [rank, mate] + far
+    yrow = [rank] + far + [mate] if rank in CFG["farfirst"] else [rank, mate] + far
 
     def make_y(lo, hi, banks):
         for k in range(lo, hi):
             j = yrow[k]
-            if k == 0:
+            if j == rank:
                 te.wait_ge(sem["q_w2"], 1)
                 te.wait_ge(sem["h_q"], 1)
-            elif k == 1:
-                te.wait_ge(sem["hn"], arrival(mate))
-            elif k == 2:
-                te.wait_ge(sem["hf"], sum(arrival(r) for r in far) if rank in HUBS else arrival(mate, 2, True))
+            elif j == mate:
+                te.wait_ge(sem["hn"], arrival(mate, 2, False))
+            elif j == far[0]:
+                te.wait_ge(sem["hf"], sum(arrival(r) for r in far) if rank in HUBS else arrival(mate))
             mm(banks[k], NC, "w2", 0, pair("h", pos[j], pos[j] + NC), "y%d_z" % j)
             out = T.oy[:, NC * j:NC * j + NC]
             (sc, ve)[k % 2].wait_ge(sem["y%d_z" % j], 1)
@@ -203,8 +184,7 @@ def rank_program(g, core, T, topo):
             stores[0] += 16
 
     def hold():
-        if CFG["hold"]:
-            sy.wait_ge(sem["sent"], sent["sent"])
+        sy.wait_ge(sem["sent"], sent["sent"])
 
     def wait_y(ks):
         for k in ks:
@@ -226,10 +206,12 @@ def rank_program(g, core, T, topo):
                 te.wait_ge(sem["h_act"], 4)
 
             def before(h):
-                if h == 0:
-                    te.wait_ge(sem["lp%d0" % m], arrival(LAST, (len(CFG["runs"]), 1)[m]))
+                if m == 0 and h == 0:
+                    te.wait_ge(sem["lp00"], arrival(LAST))
+                if m == 1 and h < CFG["p1"]:
+                    te.wait_ge(sem["lp1%d" % h], arrival(LAST, 1))
             stage("a%d" % m, "pw", "lp", NC * m, before, ([2, 3, 4, 5], [6, 7, 0, 1])[m], (T.ta, T.tb)[m], "a", NC * m)
-            hop(CFG["Q"][m], MIDDLE[m], "la", 0, "a", NC * m, "la0", ["a%d0_q" % m, "a%d1_q" % m])
+            hop(MIDDLE[m], "la", 0, "a", NC * m, "la0", ["a%d0_q" % m, "a%d1_q" % m])
         hold()
         relay_h("sent2")
         for h in range(2):
@@ -249,6 +231,8 @@ def rank_program(g, core, T, topo):
         quant("x", T.tx, 0, NC)
         quant("w1", T.tw1, 0, G * SC)
         make_h()
+        if rank in HUBS:
+            relay_h("sent")
         quant("w2", T.tw2, 0, SC)
         pre = CFG["pre"][rank]
         te.wait_ge(sem["h_act"], 4)
@@ -256,14 +240,14 @@ def rank_program(g, core, T, topo):
         w = ["pw", "lw"] if rank == 1 else ["lw", "pw"]
         te.wait_ge(sem["q_pw"], 1)
         te.wait_ge(sem["lw"], arrival(other))
-        stage("a0", w[0], "la", 0, lambda h: await_half(CFG["Q"][m], FIRST, "la0", h), [6, 7, 0, 1], T.ta, "a", 0)
+        stage("a0", w[0], "la", 0, lambda h: te.wait_ge(sem["la0%d" % h], arrival(FIRST)), [6, 7, 0, 1], T.ta, "a", 0)
         wait_y(range(pre))
         stage("b0", w[1], "a", 0, lambda h: te.wait_ge(sem["a0%d_q" % h], 1), [2, 3, 4, 5], T.tb, "b", 0)
-        hop(CFG["R"][m], LAST, "lz", NC * m, "b", 0, "lz%d" % m, ["b00_q", "b01_q"])
+        hop(LAST, "lz", NC * m, "b", 0, "lz%d" % m, ["b00_q", "b01_q"])
         hold()
         make_y(pre, 4, [6, 7, 0, 1])
     else:
-        runs = CFG["runs"]
+        runs = [(0, NC), (NC, 2 * NC)]
         for k, (a, b) in enumerate(runs):
             load("px%d" % k, T.tpx[:, 4 * a:4 * b], T.px[:, 4 * a:4 * b])
         load("x", T.tx[:], T.x[:])
@@ -271,52 +255,51 @@ def rank_program(g, core, T, topo):
         for k, (a, b) in enumerate(runs):
             quant("px", T.tpx, a, b, "px%d" % k)
             g.wait_ge(sem["q_px%d" % k], 1)
-            if a == NC:
-                part("s", FIRST, ("lp", 0, 2 * NC), ("px", 0, 2 * NC), "lp00", local="sent2")
-            part("q", FIRST, ("lp", a, b), ("px", a, b), "lp%d0" % (a // NC), local="sent2")
-        if CFG["ldhold"]:
-            sy.wait_ge(sem["sent2"], sent["sent2"])
+            if k == 1:
+                part("s", FIRST, ("lp", 0, 2 * NC), ("px", 0, 2 * NC), "lp00", "sent2")
+            n = (b - a) // (CFG["p1"] if k == 1 else 1)
+            for h in range((b - a) // n):
+                c = (a + n * h, a + n * h + n)
+                part("q", FIRST, ("lp",) + c, ("px",) + c, "lp%d%d" % (k, h), "sent2")
+        sy.wait_ge(sem["sent2"], sent["sent2"])
         load("w2", T.tw2[:], T.w2[:])
         load("pw", T.tpw[:], T.pw[:])
         quant("x", T.tx, 0, NC)
         quant("w1", T.tw1, 0, G * SC)
         make_h()
-        relay_h("sent")
         quant("w2", T.tw2, 0, SC)
         quant("pw", T.tpw, 0, G * SC)
         make_y(0, 4, [2, 3, 4, 5])
         te.wait_ge(sem["q_pw"], 1)
         te.wait_ge(sem["h_act"], 4)
         for m in range(2):
-            mode = CFG["R"][m]
-            n, parts = (HC, 2) if mode == "h" else (NC, 1)
             if m == 1:
                 wait_y(range(4))
             bks = [[6, 7, 0, 1], [2, 3, 4, 5]][m]
-            for h in range(parts):
-                await_half(mode, MIDDLE[m], "lz%d" % m, h)
+            for h in range(2):
+                te.wait_ge(sem["lz%d%d" % (m, h)], arrival(MIDDLE[m]))
+                a = NC * m + HC * h
                 for i in range(G):
-                    a = NC * m + n * h
-                    mm(bks[2 * h + i], n, "pw", i, pair("lz", a, a + n), "z%d%d_z" % (2 * m + i, h))
-            for h in range(parts):
+                    mm(bks[2 * h + i], HC, "pw", i, pair("lz", a, a + HC), "z%d%d_z" % (2 * m + i, h))
+            for h in range(2):
                 for i in range(G):
                     k = 2 * m + i
-                    out = T.oz[:, NC * k + n * h:NC * k + n * h + n]
+                    a = NC * k + HC * h
+                    out = T.oz[:, a:a + HC]
+                    (sc, ve)[i].wait_ge(sem["z%d%d_z" % (k, h)], 1)
                     if i == 0:
-                        sc.wait_ge(sem["z%d%d_z" % (k, h)], 1)
-                        sc.activation(out, bank(bks[2 * h + i], n), COPY).then_inc(sem["z%d%d_c" % (k, h)], 1)
+                        sc.activation(out, bank(bks[2 * h + i], HC), COPY).then_inc(sem["z%d%d_c" % (k, h)], 1)
                     else:
-                        ve.wait_ge(sem["z%d%d_z" % (k, h)], 1)
-                        ve.tensor_copy(out, bank(bks[2 * h + i], n)).then_inc(sem["z%d%d_c" % (k, h)], 1)
-            for i in range(G):
-                k = 2 * m + i
-                q = sc if k == 3 else sy
-                for h in range(parts):
+                        ve.tensor_copy(out, bank(bks[2 * h + i], HC)).then_inc(sem["z%d%d_c" % (k, h)], 1)
+            for h in range(2):
+                for i in range(G):
+                    k = 2 * m + i
+                    a = NC * k + HC * h
+                    q = sc if m == 1 and i == 1 and h == 1 else sy
                     q.wait_ge(sem["z%d%d_c" % (k, h)], 1)
-                q.dma_start(T.z[:, NC * k:NC * k + NC], T.oz[:, NC * k:NC * k + NC]).then_inc(
-                    sem["st_scalar" if k == 3 else "st_sync"], 16)
-                if k != 3:
-                    stores[0] += 16
+                    q.dma_start(T.z[:, a:a + HC], T.oz[:, a:a + HC]).then_inc(sem["st_scalar" if q is sc else "st_sync"], 16)
+                    if q is sy:
+                        stores[0] += 16
         sc.wait_ge(sem["st_scalar"], 16)
     sy.wait_ge(sem["st_sync"], stores[0])
     for name in sent:

@@ -7,10 +7,14 @@ HC = NC // 2
 SC = 128
 G = 2
 C = float(np.float32(0.041))
-FIRST, LAST = 0, 3
-MIDDLE = {0: 2, 1: 1}
-HUBS = (0, 1)
-CFG = {"p1": 1, "pre": {1: 3, 2: 2}, "farfirst": [1]}
+THIRD, LAST = 2, 3
+HUBS = {0: (1, 3), 3: (2, 0)}
+PRE = 1
+PX = [(0, HC), (HC, 2 * HC), (2 * HC, 3 * HC), (3 * HC, 4 * HC)]
+PX_SENDS = [(0, "q", 0, HC, "lp00"), (1, "s", 0, NC, "lp00"), (1, "q", HC, NC, "lp01"),
+            (2, "q", NC, NC + HC, "lp10"), (3, "s", NC, 2 * NC, "lp10"), (3, "q", NC + HC, 2 * NC, "lp11")]
+Z_SENDS = [(0, "q", 0, HC, "lz00"), (1, "q", HC, NC, "lz00"), (1, "s", 0, NC, "lz00"), (2, "q", NC, NC + HC, "lz10"),
+           (2, "s", NC, NC + HC, "lz10"), (3, "q", NC + HC, 2 * NC, "lz11"), (3, "s", NC + HC, 2 * NC, "lz11")]
 
 CODES = "float8_e4m3fn_x4"
 SCRATCH = {
@@ -26,14 +30,13 @@ SCRATCH = {
     "oz": ("sbuf", [128, 4 * NC], "float32"),
     "ps": ("psum", [128, 8 * 512], "float32"),
 }
-for _n, _w in (("x", NC), ("w1", G * SC), ("w2", SC), ("pw", G * SC), ("lw", G * SC), ("px", 2 * NC), ("lp", 2 * NC),
-               ("h", 4 * NC), ("a", 2 * NC), ("b", NC), ("la", NC), ("lz", 2 * NC)):
+for _n, _w in (("x", NC), ("w1", G * SC), ("w2", SC), ("pw", G * SC), ("lw", G * SC), ("px", 2 * NC), ("lp", NC),
+               ("h", 4 * NC), ("a", 2 * NC), ("b", NC), ("la", 2 * NC), ("lz", 2 * NC)):
     SCRATCH["q" + _n] = ("sbuf", [128, _w], CODES)
     SCRATCH["s" + _n] = ("sbuf", [128, _w], "uint8")
 
-SEMAPHORES = (["ld_" + n for n in ("x", "w1", "w2", "px0", "px1", "px2", "pw")]
-              + ["q_" + n for n in ("x", "w1", "w2", "px0", "px1", "px2", "pw")]
-              + ["go", "hn", "hf", "lw", "sent", "sent2", "st_sync", "st_scalar"]
+SEMAPHORES = (["%s_%s" % (e, n) for e in ("ld", "q") for n in ("x", "w1", "w2", "px0", "px1", "px2", "px3", "pw", "pw0", "pw1")]
+              + ["go", "hn", "hf0", "hf1", "hf2", "hf3", "lw", "sent", "sent2", "sent3", "st_sync", "st_scalar"]
               + ["%s%d%d" % (s, m, h) for s in ("lp", "la", "lz") for m in range(2) for h in range(2)]
               + ["%s_%s" % (s, e) for s in ("h", "a00", "a01", "a10", "a11", "b00", "b01")
                  for e in ("z0", "z1", "act", "q")]
@@ -56,9 +59,7 @@ def rank_program(g, core, T, topo):
 
     mate = [r for r in ranks if r != rank and same_chip(r, rank)][0]
     far = [r for r in ranks if not same_chip(r, rank)]
-    place = sorted(ranks, key=lambda r: (topo.chip(cores[r]), r))
-    pos = {r: NC * place.index(r) for r in ranks}
-    sent = {"sent": 0, "sent2": 0}
+    sent = {"sent": 0, "sent2": 0, "sent3": 0}
 
     def bank(k, n):
         return T.ps[:, 512 * k:512 * k + n]
@@ -75,9 +76,9 @@ def rank_program(g, core, T, topo):
             m &= ~topo.mask(cores[s], cores[[r for r in ranks if not same_chip(r, s)][0]])
         return m
 
-    def part(kind, d, dst, src, done, local="sent"):
+    def part(kind, d, dst, src, done, local="sent", everything=True):
         rid, pid = topo.addr(cores[d])[:2]
-        m = mask_of(rank, d)
+        m = mask_of(rank, d, everything)
         (dn, da, db), (sn, sa, sb) = dst, src
         out, in_ = T[kind + dn][:, da:db], T[kind + sn][:, sa:sb]
         if kind == "q":
@@ -88,21 +89,19 @@ def rank_program(g, core, T, topo):
     def arrival(s, parts=2, everything=True):
         return parts * count(mask_of(s, rank, everything))
 
-    def hop(d, dname, da, sname, sa, done, ready):
-        for h in range(2):
-            a = HC * h
-            g.wait_ge(sem[ready[h]], 1)
-            for kind in "qs":
-                part(kind, d, (dname, da + a, da + a + HC), (sname, sa + a, sa + a + HC), done + str(h))
+    def await_sends(sends, s, done, everything=True):
+        n = len([x for x in sends if x[4] == done])
+        if n:
+            te.wait_ge(sem[done], arrival(s, n, everything))
 
     def send_h():
         hub = [r for r in HUBS if r in far][0]
-        a, b = pos[rank], pos[rank] + NC
+        a, b = NC * rank, NC * rank + NC
         for k in range(2):
             def v():
                 return T.qh[:, a:b].bitcast(dt.uint8) if k == 0 else T.sh[:, a:b]
             trs = []
-            for d, done in ((hub, "hf"), (mate, "hn")):
+            for d, done in ((hub, "hf%d" % rank), (mate, "hn")):
                 rid, pid = topo.addr(cores[d])[:2]
                 m = mask_of(rank, d, False)
                 trs.append(RemoteDMATransfer(dst_ids=[DstId(rid=rid, pnc=pid)], dma_engine_mask=m,
@@ -110,11 +109,12 @@ def rank_program(g, core, T, topo):
                 sent["sent"] += count(m)
             g.remote_dma_fused(trs, local_sem=sem["sent"])
 
-    def relay_h(local):
-        a = min(pos[r] for r in far)
-        g.wait_ge(sem["hf"], sum(arrival(r) for r in far))
-        for kind in "qs":
-            part(kind, mate, ("h", a, a + 2 * NC), ("h", a, a + 2 * NC), "hf", local)
+    def relay_h():
+        for r in HUBS[rank]:
+            run = ("h", NC * r, NC * r + NC)
+            g.wait_ge(sem["hf%d" % r], arrival(r))
+            for kind in "qs":
+                part(kind, mate, run, run, "hf%d" % r, "sent2")
 
     def load(name, tile, src):
         sy.dma_start(tile, src).then_inc(sem["ld_" + name], 16)
@@ -151,16 +151,18 @@ def rank_program(g, core, T, topo):
             act("%s%d" % (ev, h), bks[2 * h], bks[2 * h + 1], HC, t, HC * h, out, oa + HC * h)
 
     def make_h():
+        quant("x", T.tx, 0, NC)
+        quant("w1", T.tw1, 0, G * SC)
         te.wait_ge(sem["q_x"], 1)
         te.wait_ge(sem["q_w1"], 1)
         for i in range(G):
             mm(i, NC, "w1", i, pair("x", 0, NC), "h_z%d" % i)
-        act("h", 0, 1, NC, T.th, 0, "h", pos[rank])
+        act("h", 0, 1, NC, T.th, 0, "h", NC * rank)
         g.wait_ge(sem["h_q"], 1)
         send_h()
 
     stores = [0]
-    yrow = [rank] + far + [mate] if rank in CFG["farfirst"] else [rank, mate] + far
+    yrow = [rank, mate] + list(HUBS[rank] if rank in HUBS else HUBS[mate])
 
     def make_y(lo, hi, banks):
         for k in range(lo, hi):
@@ -170,9 +172,9 @@ def rank_program(g, core, T, topo):
                 te.wait_ge(sem["h_q"], 1)
             elif j == mate:
                 te.wait_ge(sem["hn"], arrival(mate, 2, False))
-            elif j == far[0]:
-                te.wait_ge(sem["hf"], sum(arrival(r) for r in far) if rank in HUBS else arrival(mate))
-            mm(banks[k], NC, "w2", 0, pair("h", pos[j], pos[j] + NC), "y%d_z" % j)
+            else:
+                te.wait_ge(sem["hf%d" % j], arrival(j if rank in HUBS else mate))
+            mm(banks[k], NC, "w2", 0, pair("h", NC * j, NC * j + NC), "y%d_z" % j)
             out = T.oy[:, NC * j:NC * j + NC]
             (sc, ve)[k % 2].wait_ge(sem["y%d_z" % j], 1)
             if k % 2 == 0:
@@ -183,90 +185,103 @@ def rank_program(g, core, T, topo):
             sy.dma_start(T.y[:, NC * j:NC * j + NC], out).then_inc(sem["st_sync"], 16)
             stores[0] += 16
 
-    def hold():
-        sy.wait_ge(sem["sent"], sent["sent"])
-
     def wait_y(ks):
         for k in ks:
             te.wait_ge(sem["y%d_c" % yrow[k]], 1)
 
-    if rank == FIRST:
+    if rank not in (THIRD, LAST):
+        m, other = rank, 1 - rank
+        for i in range(G):
+            load("pw%d" % i, T.tpw[:, 512 * i:512 * i + 512], T.pw[:, 512 * i:512 * i + 512])
+        load("x", T.tx[:], T.x[:])
+        load("w1", T.tw1[:], T.w1[:])
+        load("w2", T.tw2[:], T.w2[:])
+        for i in range(G):
+            run = (SC * i, SC * i + SC)
+            quant("pw", T.tpw, run[0], run[1], "pw%d" % i)
+            g.wait_ge(sem["q_pw%d" % i], 1)
+            part("q", other, ("lw",) + run, ("pw",) + run, "lw")
+        part("s", other, ("lw", 0, G * SC), ("pw", 0, G * SC), "lw")
+        make_h()
+        w = ["lw", "lw"]
+        w[rank] = "pw"
+        te.wait_ge(sem["q_pw0"], 1)
+        te.wait_ge(sem["q_pw1"], 1)
+
+        def weights(s):
+            if w[s] == "lw":
+                te.wait_ge(sem["lw"], arrival(other, 3))
+
+        def before0(h):
+            if h == 0:
+                weights(0)
+            await_sends(PX_SENDS, LAST, "lp%d%d" % (m, h), False)
+
+        def before1(h):
+            if h == 0:
+                weights(1)
+            else:
+                te.wait_ge(sem["h_act"], 4)
+            te.wait_ge(sem["a0%d_q" % h], 1)
+        stage("a0", w[0], "lp", 0, before0, [2, 3, 4, 5], T.ta, "a", 0)
+        stage("b0", w[1], "a", 0, before1, [6, 7, 0, 1], T.tb, "b", 0)
+        for h in range(2):
+            a = HC * h
+            g.wait_ge(sem["b0%d_q" % h], 1)
+            for kind in "qs":
+                part(kind, THIRD, ("la", NC * m + a, NC * m + a + HC), ("b", a, a + HC), "la%d%d" % (m, h))
+        sy.wait_ge(sem["sent"], sent["sent"])
+        if rank in HUBS:
+            relay_h()
+        quant("w2", T.tw2, 0, SC)
+        make_y(0, 4, [2, 3, 4, 5])
+    elif rank == THIRD:
         load("x", T.tx[:], T.x[:])
         load("w1", T.tw1[:], T.w1[:])
         load("pw", T.tpw[:], T.pw[:])
         load("w2", T.tw2[:], T.w2[:])
-        quant("x", T.tx, 0, NC)
-        quant("w1", T.tw1, 0, G * SC)
         make_h()
         quant("pw", T.tpw, 0, G * SC)
         quant("w2", T.tw2, 0, SC)
+        te.wait_ge(sem["h_act"], 4)
+        make_y(0, PRE, [2, 3, 4, 5])
         te.wait_ge(sem["q_pw"], 1)
         for m in range(2):
             if m == 1:
-                te.wait_ge(sem["h_act"], 4)
-
-            def before(h):
-                if m == 0 and h == 0:
-                    te.wait_ge(sem["lp00"], arrival(LAST))
-                if m == 1 and h < CFG["p1"]:
-                    te.wait_ge(sem["lp1%d" % h], arrival(LAST, 1))
-            stage("a%d" % m, "pw", "lp", NC * m, before, ([2, 3, 4, 5], [6, 7, 0, 1])[m], (T.ta, T.tb)[m], "a", NC * m)
-            hop(MIDDLE[m], "la", 0, "a", NC * m, "la0", ["a%d0_q" % m, "a%d1_q" % m])
-        hold()
-        relay_h("sent2")
+                wait_y(range(PRE))
+            stage("a%d" % m, "pw", "la", NC * m, lambda h: te.wait_ge(sem["la%d%d" % (m, h)], arrival(m)),
+                  ([6, 7, 0, 1], [2, 3, 4, 5])[m], (T.ta, T.tb)[m], "a", NC * m)
+        for u in range(4):
+            g.wait_ge(sem["a%d%d_q" % (u // 2, u % 2)], 1)
+            for k, kind, a, b, done in Z_SENDS:
+                if k == u:
+                    part(kind, LAST, ("lz", a, b), ("a", a, b), done, "sent2" if u == 3 else "sent")
+        sy.wait_ge(sem["sent"], sent["sent"])
         for h in range(2):
             te.wait_ge(sem["a0%d_act" % h], 4)
-        make_y(0, 4, [2, 3, 4, 5])
-    elif rank != LAST:
-        m = [t for t in MIDDLE if MIDDLE[t] == rank][0]
-        other = MIDDLE[1 - m]
-        load("pw", T.tpw[:], T.pw[:])
-        load("x", T.tx[:], T.x[:])
-        load("w1", T.tw1[:], T.w1[:])
-        load("w2", T.tw2[:], T.w2[:])
-        quant("pw", T.tpw, 0, G * SC)
-        g.wait_ge(sem["q_pw"], 1)
-        for kind in "qs":
-            part(kind, other, ("lw", 0, G * SC), ("pw", 0, G * SC), "lw")
-        quant("x", T.tx, 0, NC)
-        quant("w1", T.tw1, 0, G * SC)
-        make_h()
-        if rank in HUBS:
-            relay_h("sent")
-        quant("w2", T.tw2, 0, SC)
-        pre = CFG["pre"][rank]
-        te.wait_ge(sem["h_act"], 4)
-        make_y(0, pre, [2, 3, 4, 5])
-        w = ["pw", "lw"] if rank == 1 else ["lw", "pw"]
-        te.wait_ge(sem["q_pw"], 1)
-        te.wait_ge(sem["lw"], arrival(other))
-        stage("a0", w[0], "la", 0, lambda h: te.wait_ge(sem["la0%d" % h], arrival(FIRST)), [6, 7, 0, 1], T.ta, "a", 0)
-        wait_y(range(pre))
-        stage("b0", w[1], "a", 0, lambda h: te.wait_ge(sem["a0%d_q" % h], 1), [2, 3, 4, 5], T.tb, "b", 0)
-        hop(LAST, "lz", NC * m, "b", 0, "lz%d" % m, ["b00_q", "b01_q"])
-        hold()
-        make_y(pre, 4, [6, 7, 0, 1])
+        make_y(PRE, 4, [6, 7, 0, 1])
     else:
-        runs = [(0, NC), (NC, 2 * NC)]
-        for k, (a, b) in enumerate(runs):
+        for k, (a, b) in enumerate(PX):
             load("px%d" % k, T.tpx[:, 4 * a:4 * b], T.px[:, 4 * a:4 * b])
         load("x", T.tx[:], T.x[:])
-        load("w1", T.tw1[:], T.w1[:])
-        for k, (a, b) in enumerate(runs):
+        for k, (a, b) in enumerate(PX):
             quant("px", T.tpx, a, b, "px%d" % k)
-            g.wait_ge(sem["q_px%d" % k], 1)
-            if k == 1:
-                part("s", FIRST, ("lp", 0, 2 * NC), ("px", 0, 2 * NC), "lp00", "sent2")
-            n = (b - a) // (CFG["p1"] if k == 1 else 1)
-            for h in range((b - a) // n):
-                c = (a + n * h, a + n * h + n)
-                part("q", FIRST, ("lp",) + c, ("px",) + c, "lp%d%d" % (k, h), "sent2")
-        sy.wait_ge(sem["sent2"], sent["sent2"])
+        ready = 0
+        for k, kind, a, b, done in PX_SENDS:
+            while ready <= k:
+                g.wait_ge(sem["q_px%d" % ready], 1)
+                ready += 1
+            m = a // NC
+            part(kind, m, ("lp", a - NC * m, b - NC * m), ("px", a, b), done, "sent3", False)
+        g.sem_inc(sem["go"], 1)
+        sy.wait_ge(sem["go"], 1)
+        load("w1", T.tw1[:], T.w1[:])
+        sy.wait_ge(sem["sent3"], sent["sent3"])
         load("w2", T.tw2[:], T.w2[:])
         load("pw", T.tpw[:], T.pw[:])
-        quant("x", T.tx, 0, NC)
-        quant("w1", T.tw1, 0, G * SC)
         make_h()
+        if rank in HUBS:
+            relay_h()
         quant("w2", T.tw2, 0, SC)
         quant("pw", T.tpw, 0, G * SC)
         make_y(0, 4, [2, 3, 4, 5])
@@ -277,7 +292,7 @@ def rank_program(g, core, T, topo):
                 wait_y(range(4))
             bks = [[6, 7, 0, 1], [2, 3, 4, 5]][m]
             for h in range(2):
-                te.wait_ge(sem["lz%d%d" % (m, h)], arrival(MIDDLE[m]))
+                await_sends(Z_SENDS, THIRD, "lz%d%d" % (m, h))
                 a = NC * m + HC * h
                 for i in range(G):
                     mm(bks[2 * h + i], HC, "pw", i, pair("lz", a, a + HC), "z%d%d_z" % (2 * m + i, h))
@@ -285,21 +300,20 @@ def rank_program(g, core, T, topo):
                 for i in range(G):
                     k = 2 * m + i
                     a = NC * k + HC * h
-                    out = T.oz[:, a:a + HC]
                     (sc, ve)[i].wait_ge(sem["z%d%d_z" % (k, h)], 1)
                     if i == 0:
-                        sc.activation(out, bank(bks[2 * h + i], HC), COPY).then_inc(sem["z%d%d_c" % (k, h)], 1)
+                        sc.activation(T.oz[:, a:a + HC], bank(bks[2 * h], HC), COPY).then_inc(sem["z%d%d_c" % (k, h)], 1)
                     else:
-                        ve.tensor_copy(out, bank(bks[2 * h + i], HC)).then_inc(sem["z%d%d_c" % (k, h)], 1)
-            for h in range(2):
-                for i in range(G):
-                    k = 2 * m + i
-                    a = NC * k + HC * h
-                    q = sc if m == 1 and i == 1 and h == 1 else sy
-                    q.wait_ge(sem["z%d%d_c" % (k, h)], 1)
-                    q.dma_start(T.z[:, a:a + HC], T.oz[:, a:a + HC]).then_inc(sem["st_scalar" if q is sc else "st_sync"], 16)
-                    if q is sy:
-                        stores[0] += 16
+                        ve.tensor_copy(T.oz[:, a:a + HC], bank(bks[2 * h + 1], HC)).then_inc(sem["z%d%d_c" % (k, h)], 1)
+            whole = [(0, 4, [(0, 0), (1, 0), (0, 1), (1, 1)])]
+            pieces = [(2 * i + h, 1, [(i, h)]) for h in range(2) for i in range(G)]
+            for x, (p, n, deps) in enumerate((whole, pieces)[m]):
+                q, st = (sc, "st_scalar") if m == 1 and x == 3 else (sy, "st_sync")
+                for i, h in deps:
+                    q.wait_ge(sem["z%d%d_c" % (2 * m + i, h)], 1)
+                a = 2 * NC * m + HC * p
+                q.dma_start(T.z[:, a:a + HC * n], T.oz[:, a:a + HC * n]).then_inc(sem[st], 16)
+                stores[0] += 16 if q is sy else 0
         sc.wait_ge(sem["st_scalar"], 16)
     sy.wait_ge(sem["st_sync"], stores[0])
     for name in sent:

import numpy as np
from concourse.bass import DstId, RemoteDMATransfer
from concourse.mybir import dt, AluOpType, ActivationFunctionType

NC = 256
HC = NC // 2
SC = 128
G = 2
C = float(np.float32(0.041))
THIRD, LAST = 2, 3
HUBS = {0: (1, 3), 3: (2, 0)}
PRE = 1
PX = [(0, HC), (HC, 2 * HC), (2 * HC, 3 * HC), (3 * HC, 4 * HC)]
PX_SENDS = [(0, "q", 0, HC, "lp00"), (1, "s", 0, NC, "lp00"), (1, "q", HC, NC, "lp01"),
            (2, "q", NC, NC + HC, "lp10"), (3, "s", NC, 2 * NC, "lp10"), (3, "q", NC + HC, 2 * NC, "lp11")]
Z_SENDS = [(0, "q", 0, HC, "lz00"), (1, "q", HC, NC, "lz00"), (1, "s", 0, NC, "lz00"), (2, "q", NC, NC + HC, "lz10"),
           (2, "s", NC, NC + HC, "lz10"), (3, "q", NC + HC, 2 * NC, "lz11"), (3, "s", NC + HC, 2 * NC, "lz11")]

CODES = "float8_e4m3fn_x4"
SCRATCH = {
    "tx": ("sbuf", [128, 4 * NC], "bfloat16"),
    "tw1": ("sbuf", [128, G * 512], "bfloat16"),
    "tw2": ("sbuf", [128, 512], "bfloat16"),
    "tpx": ("sbuf", [128, 2 * 4 * NC], "bfloat16"),
    "tpw": ("sbuf", [128, G * 512], "bfloat16"),
    "th": ("sbuf", [128, 4 * NC], "bfloat16"),
    "ta": ("sbuf", [128, 4 * NC], "bfloat16"),
    "tb": ("sbuf", [128, 4 * NC], "bfloat16"),
    "oy": ("sbuf", [128, 4 * NC], "float32"),
    "oz": ("sbuf", [128, 4 * NC], "float32"),
    "ps": ("psum", [128, 8 * 512], "float32"),
}
for _n, _w in (("x", NC), ("w1", G * SC), ("w2", SC), ("pw", G * SC), ("lw", G * SC), ("px", 2 * NC), ("lp", NC),
               ("h", 4 * NC), ("a", 2 * NC), ("b", NC), ("la", 2 * NC), ("lz", 2 * NC)):
    SCRATCH["q" + _n] = ("sbuf", [128, _w], CODES)
    SCRATCH["s" + _n] = ("sbuf", [128, _w], "uint8")

SEMAPHORES = (["%s_%s" % (e, n) for e in ("ld", "q") for n in ("x", "w1", "w2", "px0", "px1", "px2", "px3", "pw", "pw0", "pw1")]
              + ["go", "hn", "hf0", "hf1", "hf2", "hf3", "lw", "sent", "sent2", "sent3", "st_sync", "st_scalar"]
              + ["%s%d%d" % (s, m, h) for s in ("lp", "la", "lz") for m in range(2) for h in range(2)]
              + ["%s_%s" % (s, e) for s in ("h", "a00", "a01", "a10", "a11", "b00", "b01")
                 for e in ("z0", "z1", "act", "q")]
              + ["y%d_%s" % (j, e) for j in range(4) for e in ("z", "c")]
              + ["z%d%d_%s" % (j, h, e) for j in range(4) for h in range(2) for e in ("z", "c")])


def rank_program(g, core, T, topo):
    rank = T.rank_of(core)
    if rank is None:
        return
    sem, cores = T.sem, T.cores
    te, ve, sc, sy = g.tensor, g.vector, g.scalar, g.sync
    RELU, COPY = ActivationFunctionType.Relu, ActivationFunctionType.Copy
    MAX, MULT = AluOpType.max, AluOpType.mult
    ranks = range(len(cores))

    def same_chip(r, s):
        return topo.chip(cores[r]) == topo.chip(cores[s])

    mate = [r for r in ranks if r != rank and same_chip(r, rank)][0]
    far = [r for r in ranks if not same_chip(r, rank)]
    sent = {"sent": 0, "sent2": 0, "sent3": 0}

    def bank(k, n):
        return T.ps[:, 512 * k:512 * k + n]

    def pair(name, a, b):
        return T["q" + name][:, a:b], T["s" + name][:, a:b]

    def count(mask):
        return bin(mask).count("1")

    def mask_of(s, d, everything=True):
        m = topo.mask(cores[s], cores[d])
        if same_chip(s, d) and not everything:
            m &= ~topo.mask(cores[s], cores[[r for r in ranks if not same_chip(r, s)][0]])
        return m

    def part(kind, d, dst, src, done, local="sent", everything=True):
        rid, pid = topo.addr(cores[d])[:2]
        m = mask_of(rank, d, everything)
        (dn, da, db), (sn, sa, sb) = dst, src
        out, in_ = T[kind + dn][:, da:db], T[kind + sn][:, sa:sb]
        if kind == "q":
            out, in_ = out.bitcast(dt.uint8), in_.bitcast(dt.uint8)
        g.remote_dma(out, in_, sem[done], sem[local], pid, rid, m)
        sent[local] += count(m)

    def arrival(s, parts=2, everything=True):
        return parts * count(mask_of(s, rank, everything))

    def await_sends(sends, s, done, everything=True):
        n = len([x for x in sends if x[4] == done])
        if n:
            te.wait_ge(sem[done], arrival(s, n, everything))

    def send_h():
        hub = [r for r in HUBS if r in far][0]
        a, b = NC * rank, NC * rank + NC
        for k in range(2):
            def v():
                return T.qh[:, a:b].bitcast(dt.uint8) if k == 0 else T.sh[:, a:b]
            trs = []
            for d, done in ((hub, "hf%d" % rank), (mate, "hn")):
                rid, pid = topo.addr(cores[d])[:2]
                m = mask_of(rank, d, False)
                trs.append(RemoteDMATransfer(dst_ids=[DstId(rid=rid, pnc=pid)], dma_engine_mask=m,
                                             remote_sem=sem[done], srcs=[v()], dsts=[v()]))
                sent["sent"] += count(m)
            g.remote_dma_fused(trs, local_sem=sem["sent"])

    def relay_h():
        for r in HUBS[rank]:
            run = ("h", NC * r, NC * r + NC)
            g.wait_ge(sem["hf%d" % r], arrival(r))
            for kind in "qs":
                part(kind, mate, run, run, "hf%d" % r, "sent2")

    def load(name, tile, src):
        sy.dma_start(tile, src).then_inc(sem["ld_" + name], 16)

    def quant(name, t, a, b, tag=None):
        tag = tag or name
        ve.wait_ge(sem["ld_" + tag], 16)
        q, p = pair(name, a, b)
        ve.quantize_mx(q, p, t[:, 4 * a:4 * b]).then_inc(sem["q_" + tag], 1)

    def mm(k, n, w, i, m, ev):
        wq, wp = pair(w, SC * i, SC * i + SC)
        te.matmul_mx(bank(k, n), wq, wp, m[0], m[1], True, True).then_inc(sem[ev], 1)

    def act(ev, b0, b1, n, t, a, out, oa):
        def v(b):
            return t[:, 4 * a + b:4 * (a + n):4]
        sc.wait_ge(sem[ev + "_z0"], 1)
        sc.activation(v(0), bank(b0, n), RELU, scale=C).then_inc(sem[ev + "_act"], 1)
        sc.activation(v(1), bank(b0, n), RELU, scale=-C).then_inc(sem[ev + "_act"], 1)
        ve.wait_ge(sem[ev + "_z1"], 1)
        ve.tensor_scalar(v(2), bank(b1, n), 0.0, C, MAX, MULT).then_inc(sem[ev + "_act"], 1)
        ve.tensor_scalar(v(3), bank(b1, n), -C, 0.0, MULT, MAX).then_inc(sem[ev + "_act"], 1)
        ve.wait_ge(sem[ev + "_act"], 4)
        q, p = pair(out, oa, oa + n)
        ve.quantize_mx(q, p, t[:, 4 * a:4 * (a + n)]).then_inc(sem[ev + "_q"], 1)

    def stage(ev, w, src, sa, before, bks, t, out, oa):
        for h in range(2):
            before(h)
            s = pair(src, sa + HC * h, sa + HC * h + HC)
            for i in range(G):
                mm(bks[2 * h + i], HC, w, i, s, "%s%d_z%d" % (ev, h, i))
            act("%s%d" % (ev, h), bks[2 * h], bks[2 * h + 1], HC, t, HC * h, out, oa + HC * h)

    def make_h():
        quant("x", T.tx, 0, NC)
        quant("w1", T.tw1, 0, G * SC)
        te.wait_ge(sem["q_x"], 1)
        te.wait_ge(sem["q_w1"], 1)
        for i in range(G):
            mm(i, NC, "w1", i, pair("x", 0, NC), "h_z%d" % i)
        act("h", 0, 1, NC, T.th, 0, "h", NC * rank)
        g.wait_ge(sem["h_q"], 1)
        send_h()

    stores = [0]
    yrow = [rank, mate] + list(HUBS[rank] if rank in HUBS else HUBS[mate])

    def make_y(lo, hi, banks):
        for k in range(lo, hi):
            j = yrow[k]
            if j == rank:
                te.wait_ge(sem["q_w2"], 1)
                te.wait_ge(sem["h_q"], 1)
            elif j == mate:
                te.wait_ge(sem["hn"], arrival(mate, 2, False))
            else:
                te.wait_ge(sem["hf%d" % j], arrival(j if rank in HUBS else mate))
            mm(banks[k], NC, "w2", 0, pair("h", NC * j, NC * j + NC), "y%d_z" % j)
            out = T.oy[:, NC * j:NC * j + NC]
            (sc, ve)[k % 2].wait_ge(sem["y%d_z" % j], 1)
            if k % 2 == 0:
                sc.activation(out, bank(banks[k], NC), COPY).then_inc(sem["y%d_c" % j], 1)
            else:
                ve.tensor_copy(out, bank(banks[k], NC)).then_inc(sem["y%d_c" % j], 1)
            sy.wait_ge(sem["y%d_c" % j], 1)
            sy.dma_start(T.y[:, NC * j:NC * j + NC], out).then_inc(sem["st_sync"], 16)
            stores[0] += 16

    def wait_y(ks):
        for k in ks:
            te.wait_ge(sem["y%d_c" % yrow[k]], 1)

    if rank not in (THIRD, LAST):
        m, other = rank, 1 - rank
        for i in range(G):
            load("pw%d" % i, T.tpw[:, 512 * i:512 * i + 512], T.pw[:, 512 * i:512 * i + 512])
        load("x", T.tx[:], T.x[:])
        load("w1", T.tw1[:], T.w1[:])
        load("w2", T.tw2[:], T.w2[:])
        for i in range(G):
            run = (SC * i, SC * i + SC)
            quant("pw", T.tpw, run[0], run[1], "pw%d" % i)
            g.wait_ge(sem["q_pw%d" % i], 1)
            part("q", other, ("lw",) + run, ("pw",) + run, "lw")
        part("s", other, ("lw", 0, G * SC), ("pw", 0, G * SC), "lw")
        make_h()
        w = ["lw", "lw"]
        w[rank] = "pw"
        te.wait_ge(sem["q_pw0"], 1)
        te.wait_ge(sem["q_pw1"], 1)

        def weights(s):
            if w[s] == "lw":
                te.wait_ge(sem["lw"], arrival(other, 3))

        def before0(h):
            if h == 0:
                weights(0)
            await_sends(PX_SENDS, LAST, "lp%d%d" % (m, h), False)

        def before1(h):
            if h == 0:
                weights(1)
            else:
                te.wait_ge(sem["h_act"], 4)
            te.wait_ge(sem["a0%d_q" % h], 1)
        stage("a0", w[0], "lp", 0, before0, [2, 3, 4, 5], T.ta, "a", 0)
        stage("b0", w[1], "a", 0, before1, [6, 7, 0, 1], T.tb, "b", 0)
        for h in range(2):
            a = HC * h
            g.wait_ge(sem["b0%d_q" % h], 1)
            for kind in "qs":
                part(kind, THIRD, ("la", NC * m + a, NC * m + a + HC), ("b", a, a + HC), "la%d%d" % (m, h))
        sy.wait_ge(sem["sent"], sent["sent"])
        if rank in HUBS:
            relay_h()
        quant("w2", T.tw2, 0, SC)
        make_y(0, 4, [2, 3, 4, 5])
    elif rank == THIRD:
        load("x", T.tx[:], T.x[:])
        load("w1", T.tw1[:], T.w1[:])
        load("pw", T.tpw[:], T.pw[:])
        load("w2", T.tw2[:], T.w2[:])
        make_h()
        quant("pw", T.tpw, 0, G * SC)
        quant("w2", T.tw2, 0, SC)
        te.wait_ge(sem["h_act"], 4)
        make_y(0, PRE, [2, 3, 4, 5])
        te.wait_ge(sem["q_pw"], 1)
        for m in range(2):
            if m == 1:
                wait_y(range(PRE))
            stage("a%d" % m, "pw", "la", NC * m, lambda h: te.wait_ge(sem["la%d%d" % (m, h)], arrival(m)),
                  ([6, 7, 0, 1], [2, 3, 4, 5])[m], (T.ta, T.tb)[m], "a", NC * m)
        for u in range(4):
            g.wait_ge(sem["a%d%d_q" % (u // 2, u % 2)], 1)
            for k, kind, a, b, done in Z_SENDS:
                if k == u:
                    part(kind, LAST, ("lz", a, b), ("a", a, b), done, "sent2" if u == 3 else "sent")
        sy.wait_ge(sem["sent"], sent["sent"])
        for h in range(2):
            te.wait_ge(sem["a0%d_act" % h], 4)
        make_y(PRE, 4, [6, 7, 0, 1])
    else:
        for k, (a, b) in enumerate(PX):
            load("px%d" % k, T.tpx[:, 4 * a:4 * b], T.px[:, 4 * a:4 * b])
        load("x", T.tx[:], T.x[:])
        for k, (a, b) in enumerate(PX):
            quant("px", T.tpx, a, b, "px%d" % k)
        ready = 0
        for k, kind, a, b, done in PX_SENDS:
            while ready <= k:
                g.wait_ge(sem["q_px%d" % ready], 1)
                ready += 1
            m = a // NC
            part(kind, m, ("lp", a - NC * m, b - NC * m), ("px", a, b), done, "sent3", False)
        g.sem_inc(sem["go"], 1)
        sy.wait_ge(sem["go"], 1)
        load("w1", T.tw1[:], T.w1[:])
        sy.wait_ge(sem["sent3"], sent["sent3"])
        load("w2", T.tw2[:], T.w2[:])
        load("pw", T.tpw[:], T.pw[:])
        make_h()
        if rank in HUBS:
            relay_h()
        quant("w2", T.tw2, 0, SC)
        quant("pw", T.tpw, 0, G * SC)
        make_y(0, 4, [2, 3, 4, 5])
        te.wait_ge(sem["q_pw"], 1)
        te.wait_ge(sem["h_act"], 4)
        for m in range(2):
            if m == 1:
                wait_y(range(4))
            bks = [[6, 7, 0, 1], [2, 3, 4, 5]][m]
            for h in range(2):
                await_sends(Z_SENDS, THIRD, "lz%d%d" % (m, h))
                a = NC * m + HC * h
                for i in range(G):
                    mm(bks[2 * h + i], HC, "pw", i, pair("lz", a, a + HC), "z%d%d_z" % (2 * m + i, h))
            for h in range(2):
                for i in range(G):
                    k = 2 * m + i
                    a = NC * k + HC * h
                    (sc, ve)[i].wait_ge(sem["z%d%d_z" % (k, h)], 1)
                    if i == 0:
                        sc.activation(T.oz[:, a:a + HC], bank(bks[2 * h], HC), COPY).then_inc(sem["z%d%d_c" % (k, h)], 1)
                    else:
                        ve.tensor_copy(T.oz[:, a:a + HC], bank(bks[2 * h + 1], HC)).then_inc(sem["z%d%d_c" % (k, h)], 1)
            whole = [(0, 4, [(0, 0), (1, 0), (0, 1), (1, 1)])]
            pieces = [(2 * i + h, 1, [(i, h)]) for h in range(2) for i in range(G)]
            for x, (p, n, deps) in enumerate((whole, pieces)[m]):
                q, st = (sc, "st_scalar") if m == 1 and x == 3 else (sy, "st_sync")
                for i, h in deps:
                    q.wait_ge(sem["z%d%d_c" % (2 * m + i, h)], 1)
                a = 2 * NC * m + HC * p
                q.dma_start(T.z[:, a:a + HC * n], T.oz[:, a:a + HC * n]).then_inc(sem[st], 16)
                stores[0] += 16 if q is sy else 0
        sc.wait_ge(sem["st_scalar"], 16)
    sy.wait_ge(sem["st_sync"], stores[0])
    for name in sent:
        if sent[name]:
            g.wait_ge(sem[name], sent[name])
